import numpy as np
import ml_dtypes


def mxq(x, axis, fmt="e4m3"):
    dtype, down = {"e4m3": (ml_dtypes.float8_e4m3fn, 7), "e5m2": (ml_dtypes.float8_e5m2, 14)}[fmt]
    v = np.moveaxis(np.asarray(x, np.float32).astype(ml_dtypes.bfloat16).astype(np.float64), axis, -1)
    blocks = v.reshape(v.shape[:-1] + (-1, 32))
    amax = np.abs(blocks).max(-1, keepdims=True)
    byte = np.maximum(np.where(amax > 0, np.frexp(amax)[1] - 1 + 127, 0) - down, 1)
    scale = np.exp2(byte - 127.0)
    codes = (blocks / scale).astype(np.float32).astype(dtype).astype(np.float64)
    return np.moveaxis((codes * scale).reshape(v.shape), -1, axis)


WIDE = False


def mx_kscale(k):
    if not WIDE:
        return np.ones(k)
    levels = np.array([10, -10, 5, -5, 0])
    if k % 512:
        return np.exp2(np.random.permutation(np.resize(levels, k // 32))).repeat(32)
    a = np.empty((k // 512, 16))
    for p in range(k // 512):
        a[p, :8] = np.random.permutation(np.resize(levels, 8))
        for g in range(8):
            far = levels[np.abs(levels - a[p, g]) >= 10]
            a[p, g + 8] = far[np.random.randint(len(far))]
    return np.exp2(a.ravel()).repeat(32)


BF16 = ml_dtypes.bfloat16


def bf(x):
    return np.asarray(x, np.float32).astype(BF16)


def f64(x):
    return np.asarray(x).astype(np.float64)


E2M1 = np.array([0.0, 0.5, 1.0, 1.5, 2.0, 3.0, 4.0, 6.0, -0.0, -0.5, -1.0, -1.5, -2.0, -3.0, -4.0, -6.0])


def pack_weight(w, fmt):
    k, n = w.shape
    w = f64(bf(w)).reshape(k // 32, 32, n)
    amax = np.abs(w).max(1)
    if fmt == "e4m3":
        byte = np.frexp(amax)[1] - 1 + 127 - 7
    else:
        mant, ex = np.frexp(amax / 6.0)
        byte = np.where(mant > 0.5, ex, ex - 1) + 127
    byte = np.clip(np.where(amax > 0, byte, 1), 1, 254)
    scaled = (w * np.exp2(127.0 - byte)[:, None, :]).reshape(k, n).astype(np.float32)
    by_word = np.ascontiguousarray(scaled.reshape(k // 512, 128, 4, n).transpose(0, 1, 3, 2))
    if fmt == "e4m3":
        words = by_word.astype(ml_dtypes.float8_e4m3fn).view(np.uint8)
    else:
        c = by_word.astype(ml_dtypes.float4_e2m1fn).view(np.uint8) & 0xF
        words = c[..., 0::2] | (c[..., 1::2] << 4)
    return np.ascontiguousarray(words), np.ascontiguousarray(byte.astype(np.uint8).reshape(k // 512, 16, n))


def unpack_weight(words, scales, fmt):
    g, p, n, _ = words.shape
    if fmt == "e4m3":
        vals = np.ascontiguousarray(words).view(ml_dtypes.float8_e4m3fn).astype(np.float64)
    else:
        nib = np.empty((g, p, n, 4), np.uint8)
        nib[..., 0::2] = words & 0xF
        nib[..., 1::2] = words >> 4
        vals = E2M1[nib]
    vals = vals * np.repeat(np.exp2(scales.astype(np.float64) - 127.0), 8, axis=1)[..., None]
    return vals.transpose(0, 1, 3, 2).reshape(g * 512, n)

E4M3FN = np.array([(-1.0 if i & 128 else 1.0) * ((1.0 + (i & 7) / 8.0) * 2.0 ** (((i >> 3) & 15) - 7) if i & 120 else (i & 7) * 2.0 ** -9) for i in range(256)])


def e4m3fn_bytes(y):
    return np.clip(np.asarray(y, np.float64), -448.0, 448.0).astype(np.float32).astype(ml_dtypes.float8_e4m3fn).view(np.uint8)


def e4m3fn_values(b):
    return E4M3FN[b]


T, D, F, E, R = 1024, 1024, 1024, 128, 512


def softmax_last(l):
    m = np.max(l, axis=-1, keepdims=True)
    p = np.exp(l - m)
    return p / np.sum(p, axis=-1, keepdims=True)


def draw0():
    s, t = mx_kscale(D), mx_kscale(R)
    sd, sr = np.sqrt(D), np.sqrt(R)
    x = bf(np.random.standard_normal((T, D)) * s)
    w0_words, w0_scales = pack_weight(np.random.standard_normal((D, F)) / sd / s[:, None], "e4m3")
    wr_words, wr_scales = pack_weight(np.random.standard_normal((D, E)) / sd / s[:, None], "e4m3")
    br = bf(np.random.standard_normal(E) * 0.5)
    a_words, a_scales = pack_weight(np.random.standard_normal((D, R)) / sd / s[:, None] * t, "e4m3")
    b_words, b_scales = pack_weight(np.random.standard_normal((R, F)) * 0.6 / sr / t[:, None], "e4m3")
    return {
        "x": x,
        "w0_words": w0_words,
        "w0_scales": w0_scales,
        "wr_words": wr_words,
        "wr_scales": wr_scales,
        "br": br,
        "a_words": a_words,
        "a_scales": a_scales,
        "b_words": b_words,
        "b_scales": b_scales,
    }


def core(x, w0_words, w0_scales, wr_words, wr_scales, br, a_words, a_scales, b_words, b_scales):
    w0 = unpack_weight(w0_words, w0_scales, "e4m3")
    wr = unpack_weight(wr_words, wr_scales, "e4m3")
    a = unpack_weight(a_words, a_scales, "e4m3")
    b = unpack_weight(b_words, b_scales, "e4m3")
    n_tok = x.shape[0]
    n_exp = wr.shape[1]
    rank = a.shape[1]
    per_exp = rank // n_exp
    xq = mxq(f64(x), 1, "e4m3")
    l = (xq @ wr) + f64(br)
    g = float(n_exp) * softmax_last(l)
    u = xq @ a
    z = u.reshape(n_tok, n_exp, per_exp) * g[:, :, None]
    z = z.reshape(n_tok, rank)
    y = (xq @ w0) + (mxq(z, 1, "e4m3") @ b)
    return y


def setup_inputs():
    drawn = draw0()
    full = np.asarray(drawn['x']).astype(np.float64)
    scale = (np.abs(full).reshape(8, 128, 8, 128).max(axis=(1, 3)) / 448.0).astype(np.float32)
    given = {}
    for key, value in drawn.items():
        if key == 'x':
            given['x_bytes'] = e4m3fn_bytes(full / np.repeat(np.repeat(scale.astype(np.float64), 128, axis=0), 128, axis=1))
            given['x_scale'] = scale
        else:
            given[key] = value
    return given


def reference(x_bytes, x_scale, w0_words, w0_scales, wr_words, wr_scales, br, a_words, a_scales, b_words, b_scales):
    return core(e4m3fn_values(x_bytes) * np.repeat(np.repeat(x_scale.astype(np.float64), 128, axis=0), 128, axis=1), w0_words, w0_scales, wr_words, wr_scales, br, a_words, a_scales, b_words, b_scales)

@@ -1,0 +1,380 @@
+from contextlib import ExitStack
+
+import concourse.mybir as mybir
+from concourse.masks import make_identity
+
+T, D, F, E, R = 1024, 1024, 1024, 128, 512
+FLOPS = 2 * T * D * (F + E + R) + 2 * T * R * F
+
+F32 = mybir.dt.float32
+BF16 = mybir.dt.bfloat16
+I32 = mybir.dt.int32
+U32 = mybir.dt.uint32
+U8 = mybir.dt.uint8
+FP8 = mybir.dt.float8_e4m3fn
+FP8X4 = mybir.dt.float8_e4m3fn_x4
+MULT = mybir.AluOpType.mult
+ADD = mybir.AluOpType.add
+MAX = mybir.AluOpType.max
+AX = mybir.AxisListType.X
+ACT = mybir.ActivationFunctionType
+
+P = 128
+TILES = 8
+PAIRS = 4
+SCALAR_BLOCK = 3
+
+
+def tile_rankwisemoloradenserouter_d2p_kernel(
+    tc, x_bytes, x_scale, w0_words, w0_scales, wr_words, wr_scales, br, a_words, a_scales, b_words, b_scales, out
+):
+    nc = tc.nc
+    with ExitStack() as ctx:
+        keep = ctx.enter_context(tc.tile_pool(name="keep", bufs=1))
+        psum = ctx.enter_context(tc.psum_pool(name="psum", bufs=1))
+        ctx.enter_context(tc.manual_schedule())
+
+        a_sc_raw = keep.tile([P, 2 * R], U8, align_bytes=64, name="a_sc_raw")
+        wr_sc = keep.tile([P, 2, E], U8, align_bytes=64, name="wr_sc")
+        w0_sc = keep.tile([P, F], U8, align_bytes=64, name="w0_sc")
+        b_sc = keep.tile([P, F], U8, align_bytes=64, name="b_sc")
+        for sc in (a_sc_raw[:], wr_sc[:].rearrange("p g n -> p (g n)"), w0_sc[:], b_sc[:]):
+            nc.vector.memset(sc.bitcast(I32), 0)
+
+        zero_col = keep.tile([P, 1], F32, name="zero_col")
+        exp_col = keep.tile([P, 1], F32, name="exp_col")
+        nc.vector.memset(zero_col[:], 0.0)
+        nc.scalar.activation(out=exp_col[:], in_=zero_col[:], func=ACT.Exp)
+
+        ident = keep.tile([P, P], F32, name="ident")
+        make_identity(nc, ident[:])
+
+        x_view = x_bytes.rearrange("(p r) k -> p r k", r=TILES)
+        out_view = out.rearrange("(p r) f -> p r f", r=TILES)
+
+        scale_cols = keep.tile([P, 8], F32, name="scale_cols")
+        nc.sync.dma_start(out=scale_cols[:], in_=x_scale.unsqueeze(1).to_broadcast([8, 16, 8]))
+        xb = [keep.tile([P, 2, D], U8, align_bytes=64, name=f"xb{h}") for h in range(PAIRS)]
+
+        def load_x(h):
+            nc.sync.dma_start(out=xb[h][:], in_=x_view[:, 2 * h : 2 * h + 2, :])
+
+        load_x(0)
+        wr_c = keep.tile([P, 2, E], I32, align_bytes=64, name="wr_c")
+        nc.sync.dma_start(out=wr_c[:], in_=wr_words.rearrange("g p n t -> p g (n t)").bitcast(I32))
+        a_raw = keep.tile([P, 2, R], I32, align_bytes=64, name="a_raw")
+        nc.sync.dma_start(out=a_raw[:], in_=a_words.rearrange("g p n t -> p g (n t)").bitcast(I32))
+
+        def load_scales(tile_rows, source):
+            for q in range(4):
+                nc.sync.dma_start(out=tile_rows(q), in_=source(q))
+
+        load_scales(
+            lambda q: a_sc_raw[32 * q : 32 * q + 4, :].bitcast(I32).rearrange("p (g n) -> p g n", g=2),
+            lambda q: a_scales[:, 4 * q : 4 * q + 4, :].bitcast(I32).rearrange("g q n -> q g n"),
+        )
+        load_scales(
+            lambda q: wr_sc[32 * q : 32 * q + 4, :, :].bitcast(I32),
+            lambda q: wr_scales[:, 4 * q : 4 * q + 4, :].bitcast(I32).rearrange("g q n -> q g n"),
+        )
+        br_bc = keep.tile([P, E], BF16, name="br_bc")
+        nc.gpsimd.dma_start(out=br_bc[:], in_=br.partition_broadcast(P))
+        load_x(1)
+        w0_view = w0_words.rearrange("g p n t -> p g (n t)")
+        w0_c = [keep.tile([P, 2, 512], I32, align_bytes=64, name=f"w0_c{f}") for f in range(2)]
+        nc.sync.dma_start(out=w0_c[0][:], in_=w0_view[:, :, 0:2048].bitcast(I32))
+        load_scales(
+            lambda q: w0_sc[32 * q : 32 * q + 8, :].bitcast(I32),
+            lambda q: w0_scales[:, 4 * q : 4 * q + 4, :].bitcast(I32),
+        )
+        nc.sync.dma_start(out=w0_c[1][:], in_=w0_view[:, :, 2048:4096].bitcast(I32))
+        b_c = keep.tile([P, F], I32, align_bytes=64, name="b_c")
+        nc.sync.dma_start(out=b_c[:], in_=b_words[0].rearrange("p n t -> p (n t)").bitcast(I32))
+        load_scales(
+            lambda q: b_sc[32 * q : 32 * q + 4, :].bitcast(I32),
+            lambda q: b_scales[0, 4 * q : 4 * q + 4, :].bitcast(I32),
+        )
+        load_x(2)
+        load_x(3)
+
+        xw = [keep.tile([P, D], BF16, align_bytes=64, name=f"xw{r}") for r in range(TILES)]
+        xg = [keep.tile([P, 2 * P * 4], BF16, align_bytes=64, name=f"xg{r}") for r in range(TILES)]
+        xq = [keep.tile([P, 2 * P], U32, align_bytes=64, name=f"xq{r}") for r in range(TILES)]
+        xs = [keep.tile([P, 2 * P], U8, align_bytes=64, name=f"xs{r}") for r in range(TILES)]
+        zb = [keep.tile([P, P, 4], BF16, align_bytes=64, name=f"zb{r}") for r in range(TILES)]
+        zq = [keep.tile([P, P], U32, align_bytes=64, name=f"zq{r}") for r in range(TILES)]
+        zs = [keep.tile([P, P], U8, align_bytes=64, name=f"zs{r}") for r in range(TILES)]
+        yo = [keep.tile([P, F], F32, align_bytes=64, name=f"yo{r}") for r in range(TILES)]
+        lb = [keep.tile([P, 2, E], F32, name=f"lb{h}") for h in range(PAIRS)]
+        ex = [keep.tile([P, 2, E], F32, name=f"ex{h}") for h in range(PAIRS)]
+        gt = [keep.tile([P, 2, E], F32, name=f"gt{h}") for h in range(PAIRS)]
+        gs = [keep.tile([P, 2, P], F32, name=f"gs{h}") for h in range(PAIRS)]
+        nm = [keep.tile([P, 2], F32, name=f"nm{h}") for h in range(PAIRS)]
+        sm = [keep.tile([P, 2], F32, name=f"sm{h}") for h in range(PAIRS)]
+        rs = [keep.tile([P, 2], F32, name=f"rs{h}") for h in range(PAIRS)]
+        a_c = keep.tile([P, 2, 4, P], I32, align_bytes=64, name="a_c")
+        a_sc = keep.tile([P, 2, 4, P], U8, align_bytes=64, name="a_sc")
+        u_ps = {}
+        y_ps = {}
+        l_ps = {}
+        g_ps = {}
+        t_ps = {}
+
+        def widen_vector(r):
+            for j in range(8):
+                if j % 4 != SCALAR_BLOCK:
+                    cols = slice(P * j, P * j + P)
+                    nc.vector.tensor_scalar(
+                        out=xw[r][:, cols],
+                        in0=xb[r // 2][:, r % 2, cols].bitcast(FP8),
+                        scalar1=scale_cols[:, j : j + 1],
+                        scalar2=None,
+                        op0=MULT,
+                    )
+
+        def widen_scalar(r):
+            for j in range(8):
+                if j % 4 == SCALAR_BLOCK:
+                    cols = slice(P * j, P * j + P)
+                    nc.scalar.activation(
+                        out=xw[r][:, cols],
+                        in_=xb[r // 2][:, r % 2, cols].bitcast(FP8),
+                        func=ACT.Copy,
+                        scale=scale_cols[:, j : j + 1],
+                    )
+
+        def turn(r):
+            t_ps[r] = psum.tile([P, 4, P], F32, tag="tr", bufs=2, name=f"t_ps{r}")
+            words = xw[r][:].bitcast(F32)
+            for g in range(2):
+                for u in range(2):
+                    nc.tensor.transpose(
+                        t_ps[r][:, 2 * g + u, :], words[:, 256 * g + u : 256 * (g + 1) : 2], ident[:]
+                    )
+
+        def interleave(r):
+            nc.scalar.copy(
+                out=xg[r][:].bitcast(F32).rearrange("p (g n u) -> p g n u", g=2, u=2),
+                in_=t_ps[r][:].rearrange("p (g u) n -> p g n u", g=2),
+            )
+
+        def quantize_x(r):
+            nc.vector.quantize_mx(out=xq[r][:].bitcast(FP8X4), scales=xs[r][:], in_=xg[r][:])
+
+        def xq_of(r, g):
+            return xq[r][:, P * g : P * g + P].bitcast(FP8X4), xs[r][:, P * g : P * g + P]
+
+        def logits(h):
+            l_ps[h] = psum.tile([P, 2, E], F32, tag="lg", bufs=1, name=f"l_ps{h}")
+            for i in range(2):
+                for g in range(2):
+                    codes, scales = xq_of(2 * h + i, g)
+                    nc.tensor.matmul_mx(
+                        out=l_ps[h][:, i, :],
+                        lhsT=codes,
+                        lhsT_scale=scales,
+                        rhs=wr_c[:, g, :].bitcast(FP8X4),
+                        rhs_scale=wr_sc[:, g, :],
+                        start=(g == 0),
+                        stop=(g == 1),
+                    )
+
+        def down(r):
+            u_ps[r] = psum.tile([P, 4, P], F32, tag="u", bufs=2, name=f"u_ps{r}")
+            for t in range(4):
+                for g in range(2):
+                    codes, scales = xq_of(r, g)
+                    nc.tensor.matmul_mx(
+                        out=u_ps[r][:, t, :],
+                        lhsT=a_c[:, g, t, :].bitcast(FP8X4),
+                        lhsT_scale=a_sc[:, g, t, :],
+                        rhs=codes,
+                        rhs_scale=scales,
+                        start=(g == 0),
+                        stop=(g == 1),
+                    )
+
+        def soft_max(h):
+            nc.vector.tensor_tensor(
+                out=lb[h][:], in0=l_ps[h][:], in1=br_bc[:].unsqueeze(1).to_broadcast([P, 2, E]), op=ADD
+            )
+            nc.vector.tensor_reduce(out=nm[h][:], in_=lb[h][:], axis=AX, op=MAX, negate=True)
+
+        def soft_exp(h):
+            for i in range(2):
+                nc.scalar.activation(
+                    out=ex[h][:, i, :],
+                    in_=lb[h][:, i, :],
+                    func=ACT.Exp,
+                    bias=nm[h][:, i : i + 1],
+                    accum_out=sm[h][:, i : i + 1],
+                )
+
+        def soft_scale(h):
+            nc.vector.reciprocal(out=rs[h][:], in_=sm[h][:])
+            for i in range(2):
+                nc.vector.tensor_scalar(
+                    out=gt[h][:, i, :],
+                    in0=ex[h][:, i, :],
+                    scalar1=rs[h][:, i : i + 1],
+                    scalar2=float(E),
+                    op0=MULT,
+                    op1=MULT,
+                )
+
+        def turn_gates(h):
+            g_ps[h] = psum.tile([P, 2, P], F32, tag="lg", bufs=1, name=f"g_ps{h}")
+            for i in range(2):
+                nc.tensor.transpose(g_ps[h][:, i, :], gt[h][:, i, :], ident[:])
+
+        def copy_gates(h):
+            nc.scalar.copy(out=gs[h][:], in_=g_ps[h][:])
+
+        def gate(r):
+            nc.vector.tensor_tensor(
+                out=zb[r][:],
+                in0=u_ps[r][:].rearrange("p t n -> p n t"),
+                in1=gs[r // 2][:, r % 2, :].unsqueeze(2).to_broadcast([P, P, 4]),
+                op=MULT,
+            )
+
+        def quantize_z(r):
+            nc.vector.quantize_mx(
+                out=zq[r][:].bitcast(FP8X4), scales=zs[r][:], in_=zb[r][:].rearrange("p n t -> p (n t)")
+            )
+
+        def base(r, c0, width, tag, bufs):
+            y_ps[r, c0] = psum.tile([P, width], F32, tag=tag, bufs=bufs, name=f"y_ps{r}_{c0}")
+            f, c = c0 // 512, c0 % 512
+            for g in range(2):
+                codes, scales = xq_of(r, g)
+                nc.tensor.matmul_mx(
+                    out=y_ps[r, c0][:],
+                    lhsT=codes,
+                    lhsT_scale=scales,
+                    rhs=w0_c[f][:, g, c : c + width].bitcast(FP8X4),
+                    rhs_scale=w0_sc[4 * g :, c0 : c0 + width],
+                    start=(g == 0),
+                    stop=False,
+                )
+
+        def lora(r, c0, width):
+            nc.tensor.matmul_mx(
+                out=y_ps[r, c0][:],
+                lhsT=zq[r][:].bitcast(FP8X4),
+                lhsT_scale=zs[r][:],
+                rhs=b_c[:, c0 : c0 + width].bitcast(FP8X4),
+                rhs_scale=b_sc[:, c0 : c0 + width],
+                start=False,
+                stop=True,
+            )
+
+        def empty(r, c0, width, engine_copy):
+            engine_copy(out=yo[r][:, c0 : c0 + width], in_=y_ps[r, c0][:])
+
+        def store(r, c0, width):
+            nc.sync.dma_start(out=out_view[:, r, c0 : c0 + width], in_=yo[r][:, c0 : c0 + width])
+
+        def out_tile(r, tag, bufs):
+            base(r, 0, 512, tag, bufs)
+            base(r, 512, 512, tag, bufs)
+            lora(r, 0, 512)
+            lora(r, 512, 512)
+
+        v_copy = nc.vector.tensor_copy
+        s_copy = nc.scalar.copy
+
+        for r in (0, 1):
+            widen_vector(r)
+            widen_scalar(r)
+        turn(0)
+        turn(1)
+        interleave(0)
+        interleave(1)
+        nc.vector.tensor_copy(
+            out=a_c[:], in_=a_raw[:].rearrange("p g (m t) -> p g t m", t=4)
+        )
+        quantize_x(0)
+        nc.vector.tensor_copy(
+            out=a_sc[:], in_=a_sc_raw[:].rearrange("p (g m t) -> p g t m", g=2, t=4)
+        )
+        quantize_x(1)
+        logits(0)
+        down(0)
+        down(1)
+        widen_scalar(2)
+        widen_scalar(3)
+        soft_max(0)
+        widen_vector(2)
+        widen_vector(3)
+        soft_exp(0)
+        soft_scale(0)
+        turn(2)
+        turn(3)
+        turn_gates(0)
+        interleave(2)
+        copy_gates(0)
+        interleave(3)
+        quantize_x(2)
+        gate(0)
+        gate(1)
+        quantize_x(3)
+        quantize_z(0)
+        quantize_z(1)
+        for h in range(PAIRS):
+            r0, r1 = 2 * h, 2 * h + 1
+            more = h + 1 < PAIRS
+            load_ahead = h + 2 < PAIRS
+            if load_ahead:
+                widen_scalar(2 * h + 4)
+                widen_scalar(2 * h + 5)
+            if more:
+                logits(h + 1)
+                down(2 * h + 2)
+                down(2 * h + 3)
+                soft_max(h + 1)
+                if load_ahead:
+                    widen_vector(2 * h + 4)
+                    widen_vector(2 * h + 5)
+                soft_exp(h + 1)
+                soft_scale(h + 1)
+                out_tile(r0, "y", 3)
+                empty(r0, 0, 512, s_copy)
+                empty(r0, 512, 512, v_copy)
+                store(r0, 0, F)
+                turn_gates(h + 1)
+                copy_gates(h + 1)
+                if load_ahead:
+                    turn(2 * h + 4)
+                    turn(2 * h + 5)
+                    interleave(2 * h + 4)
+                    interleave(2 * h + 5)
+                gate(2 * h + 2)
+                gate(2 * h + 3)
+                if load_ahead:
+                    quantize_x(2 * h + 4)
+                quantize_z(2 * h + 2)
+                if load_ahead:
+                    quantize_x(2 * h + 5)
+                quantize_z(2 * h + 3)
+                out_tile(r1, "y", 3)
+                empty(r1, 0, 512, s_copy)
+                empty(r1, 512, 512, s_copy)
+                store(r1, 0, F)
+            else:
+                out_tile(r0, "tr", 2)
+                empty(r0, 0, 512, s_copy)
+                empty(r0, 512, 512, v_copy)
+                store(r0, 0, F)
+                base(r1, 0, 512, "y", 3)
+                lora(r1, 0, 512)
+                empty(r1, 0, 512, s_copy)
+                store(r1, 0, 512)
+                base(r1, 512, 256, "y", 3)
+                lora(r1, 512, 256)
+                empty(r1, 512, 256, v_copy)
+                store(r1, 512, 256)
+                base(r1, 768, 256, "y", 3)
+                lora(r1, 768, 256)
+                empty(r1, 768, 256, s_copy)
+                store(r1, 768, 256)

@@ -22,7 +22,11 @@ ACT = mybir.ActivationFunctionType
 P = 128
 TILES = 8
 PAIRS = 4
-SCALAR_BLOCK = 3
+S_BLOCKS = {0: (2, 3, 7), 1: (2, 3, 7), 2: (1, 3, 5, 7), 3: (1, 3, 5, 7)}
+CONTIG = (4, 5, 6, 7)
+G_A = ()
+Y_V = ((2, 512), (4, 512), (6, 512), (7, 512))
+G_B = (0, 1, 2, 3)
 
 
 def tile_rankwisemoloradenserouter_d2p_kernel(
@@ -46,54 +50,72 @@ def tile_rankwisemoloradenserouter_d2p_kernel(
         nc.vector.memset(zero_col[:], 0.0)
         nc.scalar.activation(out=exp_col[:], in_=zero_col[:], func=ACT.Exp)
 
-        ident = keep.tile([P, P], F32, name="ident")
-        make_identity(nc, ident[:])
-
         x_view = x_bytes.rearrange("(p r) k -> p r k", r=TILES)
         out_view = out.rearrange("(p r) f -> p r f", r=TILES)
+        w0_view = w0_words.rearrange("g p n t -> p g (n t)")
 
+        ident = keep.tile([P, P], F32, name="ident")
+        nc.vector.memset(ident[:], 0.0)
         scale_cols = keep.tile([P, 8], F32, name="scale_cols")
-        nc.sync.dma_start(out=scale_cols[:], in_=x_scale.unsqueeze(1).to_broadcast([8, 16, 8]))
         xb = [keep.tile([P, 2, D], U8, align_bytes=64, name=f"xb{h}") for h in range(PAIRS)]
+        wr_c = keep.tile([P, 2, E], I32, align_bytes=64, name="wr_c")
+        a_raw = keep.tile([P, 2, R], I32, align_bytes=64, name="a_raw")
+        b_c = keep.tile([P, F], I32, align_bytes=64, name="b_c")
+        br_bc = keep.tile([P, E], BF16, name="br_bc")
+        w0_c = [keep.tile([P, 2, 512], I32, align_bytes=64, name=f"w0_c{f}") for f in range(2)]
 
         def load_x(h):
             nc.sync.dma_start(out=xb[h][:], in_=x_view[:, 2 * h : 2 * h + 2, :])
 
+        def load_w0(f):
+            nc.sync.dma_start(out=w0_c[f][:], in_=w0_view[:, :, 2048 * f : 2048 * f + 2048].bitcast(I32))
+
+        def wr_scale(queue, q):
+            queue.dma_start(
+                out=wr_sc[32 * q : 32 * q + 4, :, :].bitcast(I32),
+                in_=wr_scales[:, 4 * q : 4 * q + 4, :].bitcast(I32).rearrange("g q n -> q g n"),
+            )
+
+        def a_scale(queue, q):
+            queue.dma_start(
+                out=a_sc_raw[32 * q : 32 * q + 4, :].bitcast(I32).rearrange("p (g n) -> p g n", g=2),
+                in_=a_scales[:, 4 * q : 4 * q + 4, :].bitcast(I32).rearrange("g q n -> q g n"),
+            )
+
+        def w0_scale(queue, q):
+            queue.dma_start(
+                out=w0_sc[32 * q : 32 * q + 8, :].bitcast(I32), in_=w0_scales[:, 4 * q : 4 * q + 4, :].bitcast(I32)
+            )
+
+        def b_scale(queue, q):
+            queue.dma_start(
+                out=b_sc[32 * q : 32 * q + 4, :].bitcast(I32), in_=b_scales[0, 4 * q : 4 * q + 4, :].bitcast(I32)
+            )
+
         load_x(0)
-        wr_c = keep.tile([P, 2, E], I32, align_bytes=64, name="wr_c")
-        nc.sync.dma_start(out=wr_c[:], in_=wr_words.rearrange("g p n t -> p g (n t)").bitcast(I32))
-        a_raw = keep.tile([P, 2, R], I32, align_bytes=64, name="a_raw")
-        nc.sync.dma_start(out=a_raw[:], in_=a_words.rearrange("g p n t -> p g (n t)").bitcast(I32))
-
-        def load_scales(tile_rows, source):
-            for q in range(4):
-                nc.sync.dma_start(out=tile_rows(q), in_=source(q))
-
-        load_scales(
-            lambda q: a_sc_raw[32 * q : 32 * q + 4, :].bitcast(I32).rearrange("p (g n) -> p g n", g=2),
-            lambda q: a_scales[:, 4 * q : 4 * q + 4, :].bitcast(I32).rearrange("g q n -> q g n"),
-        )
-        load_scales(
-            lambda q: wr_sc[32 * q : 32 * q + 4, :, :].bitcast(I32),
-            lambda q: wr_scales[:, 4 * q : 4 * q + 4, :].bitcast(I32).rearrange("g q n -> q g n"),
-        )
-        br_bc = keep.tile([P, E], BF16, name="br_bc")
+        nc.sync.dma_start(out=scale_cols[:], in_=x_scale.unsqueeze(1).to_broadcast([8, 16, 8]))
+        for q in G_A:
+            a_scale(nc.gpsimd, q)
+        make_identity(nc, ident[:], nomemset=True)
         nc.gpsimd.dma_start(out=br_bc[:], in_=br.partition_broadcast(P))
+        for q in G_B:
+            b_scale(nc.gpsimd, q)
+        for q in range(4):
+            wr_scale(nc.sync, q)
+        nc.sync.dma_start(out=wr_c[:], in_=wr_words.rearrange("g p n t -> p g (n t)").bitcast(I32))
+        nc.sync.dma_start(out=a_raw[:], in_=a_words.rearrange("g p n t -> p g (n t)").bitcast(I32))
+        for q in range(4):
+            if q not in G_A:
+                a_scale(nc.sync, q)
         load_x(1)
-        w0_view = w0_words.rearrange("g p n t -> p g (n t)")
-        w0_c = [keep.tile([P, 2, 512], I32, align_bytes=64, name=f"w0_c{f}") for f in range(2)]
-        nc.sync.dma_start(out=w0_c[0][:], in_=w0_view[:, :, 0:2048].bitcast(I32))
-        load_scales(
-            lambda q: w0_sc[32 * q : 32 * q + 8, :].bitcast(I32),
-            lambda q: w0_scales[:, 4 * q : 4 * q + 4, :].bitcast(I32),
-        )
-        nc.sync.dma_start(out=w0_c[1][:], in_=w0_view[:, :, 2048:4096].bitcast(I32))
-        b_c = keep.tile([P, F], I32, align_bytes=64, name="b_c")
+        load_w0(0)
+        load_w0(1)
+        for q in range(4):
+            w0_scale(nc.sync, q)
         nc.sync.dma_start(out=b_c[:], in_=b_words[0].rearrange("p n t -> p (n t)").bitcast(I32))
-        load_scales(
-            lambda q: b_sc[32 * q : 32 * q + 4, :].bitcast(I32),
-            lambda q: b_scales[0, 4 * q : 4 * q + 4, :].bitcast(I32),
-        )
+        for q in range(4):
+            if q not in G_B:
+                b_scale(nc.sync, q)
         load_x(2)
         load_x(3)
 
@@ -122,19 +144,24 @@ def tile_rankwisemoloradenserouter_d2p_kernel(
 
         def widen_vector(r):
             for j in range(8):
-                if j % 4 != SCALAR_BLOCK:
-                    cols = slice(P * j, P * j + P)
-                    nc.vector.tensor_scalar(
-                        out=xw[r][:, cols],
-                        in0=xb[r // 2][:, r % 2, cols].bitcast(FP8),
-                        scalar1=scale_cols[:, j : j + 1],
-                        scalar2=None,
-                        op0=MULT,
-                    )
+                cols = slice(P * j, P * j + P)
+                if r in CONTIG:
+                    dest = xw[r][:].rearrange("p (g u q e) -> p g q u e", g=2, u=2, e=2)[
+                        :, j // 4, 32 * (j % 4) : 32 * (j % 4) + 32
+                    ]
+                    source = xb[r // 2][:, r % 2, cols].bitcast(FP8).rearrange("p (q u e) -> p q u e", u=2, e=2)
+                elif j not in S_BLOCKS[r]:
+                    dest = xw[r][:, cols]
+                    source = xb[r // 2][:, r % 2, cols].bitcast(FP8)
+                else:
+                    continue
+                nc.vector.tensor_scalar(
+                    out=dest, in0=source, scalar1=scale_cols[:, j : j + 1], scalar2=None, op0=MULT
+                )
 
         def widen_scalar(r):
             for j in range(8):
-                if j % 4 == SCALAR_BLOCK:
+                if r not in CONTIG and j in S_BLOCKS[r]:
                     cols = slice(P * j, P * j + P)
                     nc.scalar.activation(
                         out=xw[r][:, cols],
@@ -148,9 +175,11 @@ def tile_rankwisemoloradenserouter_d2p_kernel(
             words = xw[r][:].bitcast(F32)
             for g in range(2):
                 for u in range(2):
-                    nc.tensor.transpose(
-                        t_ps[r][:, 2 * g + u, :], words[:, 256 * g + u : 256 * (g + 1) : 2], ident[:]
-                    )
+                    if r in CONTIG:
+                        part = words[:, 256 * g + P * u : 256 * g + P * u + P]
+                    else:
+                        part = words[:, 256 * g + u : 256 * (g + 1) : 2]
+                    nc.tensor.transpose(t_ps[r][:, 2 * g + u, :], part, ident[:])
 
         def interleave(r):
             nc.scalar.copy(
@@ -164,20 +193,21 @@ def tile_rankwisemoloradenserouter_d2p_kernel(
         def xq_of(r, g):
             return xq[r][:, P * g : P * g + P].bitcast(FP8X4), xs[r][:, P * g : P * g + P]
 
-        def logits(h):
-            l_ps[h] = psum.tile([P, 2, E], F32, tag="lg", bufs=1, name=f"l_ps{h}")
-            for i in range(2):
-                for g in range(2):
-                    codes, scales = xq_of(2 * h + i, g)
-                    nc.tensor.matmul_mx(
-                        out=l_ps[h][:, i, :],
-                        lhsT=codes,
-                        lhsT_scale=scales,
-                        rhs=wr_c[:, g, :].bitcast(FP8X4),
-                        rhs_scale=wr_sc[:, g, :],
-                        start=(g == 0),
-                        stop=(g == 1),
-                    )
+        def logits(r):
+            h, i = r // 2, r % 2
+            if i == 0:
+                l_ps[h] = psum.tile([P, 2, E], F32, tag="lg", bufs=1, name=f"l_ps{h}")
+            for g in range(2):
+                codes, scales = xq_of(r, g)
+                nc.tensor.matmul_mx(
+                    out=l_ps[h][:, i, :],
+                    lhsT=codes,
+                    lhsT_scale=scales,
+                    rhs=wr_c[:, g, :].bitcast(FP8X4),
+                    rhs_scale=wr_sc[:, g, :],
+                    start=(g == 0),
+                    stop=(g == 1),
+                )
 
         def down(r):
             u_ps[r] = psum.tile([P, 4, P], F32, tag="u", bufs=2, name=f"u_ps{r}")
@@ -232,9 +262,9 @@ def tile_rankwisemoloradenserouter_d2p_kernel(
 
         def gate(r):
             nc.vector.tensor_tensor(
-                out=zb[r][:],
-                in0=u_ps[r][:].rearrange("p t n -> p n t"),
-                in1=gs[r // 2][:, r % 2, :].unsqueeze(2).to_broadcast([P, P, 4]),
+                out=zb[r][:].rearrange("p (c i) t -> p c t i", i=4),
+                in0=u_ps[r][:].rearrange("p t (c i) -> p c t i", i=4),
+                in1=gs[r // 2][:, r % 2, :].rearrange("p (c i) -> p c i", i=4).unsqueeze(2).to_broadcast([P, 32, 4, 4]),
                 op=MULT,
             )
 
@@ -269,112 +299,171 @@ def tile_rankwisemoloradenserouter_d2p_kernel(
                 stop=True,
             )
 
-        def empty(r, c0, width, engine_copy):
+        def empty(r, c0, width):
+            engine_copy = nc.vector.tensor_copy if (r, c0) in Y_V else nc.scalar.copy
             engine_copy(out=yo[r][:, c0 : c0 + width], in_=y_ps[r, c0][:])
 
         def store(r, c0, width):
             nc.sync.dma_start(out=out_view[:, r, c0 : c0 + width], in_=yo[r][:, c0 : c0 + width])
 
-        def out_tile(r, tag, bufs):
+        def perm_words():
+            nc.vector.tensor_copy(out=a_c[:], in_=a_raw[:].rearrange("p g (m t) -> p g t m", t=4))
+
+        def perm_scales():
+            nc.vector.tensor_copy(out=a_sc[:], in_=a_sc_raw[:].rearrange("p (g m t) -> p g t m", g=2, t=4))
+
+        def bases(r, tag, bufs):
             base(r, 0, 512, tag, bufs)
             base(r, 512, 512, tag, bufs)
-            lora(r, 0, 512)
-            lora(r, 512, 512)
 
-        v_copy = nc.vector.tensor_copy
-        s_copy = nc.scalar.copy
-
-        for r in (0, 1):
-            widen_vector(r)
-            widen_scalar(r)
+        widen_vector(0)
+        widen_scalar(0)
         turn(0)
+        widen_vector(1)
+        widen_scalar(1)
+        perm_words()
         turn(1)
         interleave(0)
-        interleave(1)
-        nc.vector.tensor_copy(
-            out=a_c[:], in_=a_raw[:].rearrange("p g (m t) -> p g t m", t=4)
-        )
         quantize_x(0)
-        nc.vector.tensor_copy(
-            out=a_sc[:], in_=a_sc_raw[:].rearrange("p (g m t) -> p g t m", g=2, t=4)
-        )
-        quantize_x(1)
+        interleave(1)
+        perm_scales()
         logits(0)
-        down(0)
-        down(1)
-        widen_scalar(2)
         widen_scalar(3)
-        soft_max(0)
+        quantize_x(1)
+        widen_scalar(2)
         widen_vector(2)
+        logits(1)
+        down(0)
+        soft_max(0)
+        turn(2)
         widen_vector(3)
         soft_exp(0)
-        soft_scale(0)
-        turn(2)
         turn(3)
-        turn_gates(0)
+        soft_scale(0)
         interleave(2)
-        copy_gates(0)
+        turn_gates(0)
         interleave(3)
+        down(1)
         quantize_x(2)
-        gate(0)
-        gate(1)
+        copy_gates(0)
         quantize_x(3)
+        base(0, 0, 512, "y", 3)
+        gate(0)
+        logits(2)
+        logits(3)
+        gate(1)
+        base(0, 512, 512, "y", 3)
         quantize_z(0)
+        down(2)
+        soft_max(1)
+        down(3)
+        widen_vector(4)
+        soft_exp(1)
+        lora(0, 0, 512)
+        lora(0, 512, 512)
+        soft_scale(1)
+        turn(4)
+        empty(0, 512, 512)
+        widen_vector(5)
+        turn_gates(1)
+        base(1, 0, 512, "y", 3)
+        copy_gates(1)
         quantize_z(1)
-        for h in range(PAIRS):
-            r0, r1 = 2 * h, 2 * h + 1
-            more = h + 1 < PAIRS
-            load_ahead = h + 2 < PAIRS
-            if load_ahead:
-                widen_scalar(2 * h + 4)
-                widen_scalar(2 * h + 5)
-            if more:
-                logits(h + 1)
-                down(2 * h + 2)
-                down(2 * h + 3)
-                soft_max(h + 1)
-                if load_ahead:
-                    widen_vector(2 * h + 4)
-                    widen_vector(2 * h + 5)
-                soft_exp(h + 1)
-                soft_scale(h + 1)
-                out_tile(r0, "y", 3)
-                empty(r0, 0, 512, s_copy)
-                empty(r0, 512, 512, v_copy)
-                store(r0, 0, F)
-                turn_gates(h + 1)
-                copy_gates(h + 1)
-                if load_ahead:
-                    turn(2 * h + 4)
-                    turn(2 * h + 5)
-                    interleave(2 * h + 4)
-                    interleave(2 * h + 5)
-                gate(2 * h + 2)
-                gate(2 * h + 3)
-                if load_ahead:
-                    quantize_x(2 * h + 4)
-                quantize_z(2 * h + 2)
-                if load_ahead:
-                    quantize_x(2 * h + 5)
-                quantize_z(2 * h + 3)
-                out_tile(r1, "y", 3)
-                empty(r1, 0, 512, s_copy)
-                empty(r1, 512, 512, s_copy)
-                store(r1, 0, F)
-            else:
-                out_tile(r0, "tr", 2)
-                empty(r0, 0, 512, s_copy)
-                empty(r0, 512, 512, v_copy)
-                store(r0, 0, F)
-                base(r1, 0, 512, "y", 3)
-                lora(r1, 0, 512)
-                empty(r1, 0, 512, s_copy)
-                store(r1, 0, 512)
-                base(r1, 512, 256, "y", 3)
-                lora(r1, 512, 256)
-                empty(r1, 512, 256, v_copy)
-                store(r1, 512, 256)
-                base(r1, 768, 256, "y", 3)
-                lora(r1, 768, 256)
-                empty(r1, 768, 256, s_copy)
-                store(r1, 768, 256)
+        empty(0, 0, 512)
+        gate(2)
+        turn(5)
+        interleave(4)
+        store(0, 0, 1024)
+        base(1, 512, 512, "y", 3)
+        gate(3)
+        interleave(5)
+        quantize_x(4)
+        lora(1, 0, 512)
+        lora(1, 512, 512)
+        quantize_x(5)
+        empty(1, 0, 512)
+        base(2, 0, 512, "y", 3)
+        widen_vector(6)
+        logits(4)
+        logits(5)
+        down(4)
+        soft_max(2)
+        down(5)
+        quantize_z(2)
+        soft_exp(2)
+        base(2, 512, 512, "y", 3)
+        empty(1, 512, 512)
+        soft_scale(2)
+        lora(2, 0, 512)
+        widen_vector(7)
+        lora(2, 512, 512)
+        empty(2, 0, 512)
+        turn_gates(2)
+        quantize_z(3)
+        turn(6)
+        empty(2, 512, 512)
+        copy_gates(2)
+        turn(7)
+        interleave(6)
+        base(3, 0, 512, "y", 3)
+        gate(4)
+        interleave(7)
+        quantize_x(6)
+        base(3, 512, 512, "y", 3)
+        quantize_x(7)
+        lora(3, 0, 512)
+        quantize_z(4)
+        lora(3, 512, 512)
+        gate(5)
+        empty(3, 0, 512)
+        down(6)
+        empty(3, 512, 512)
+        logits(6)
+        logits(7)
+        base(4, 0, 512, "y", 3)
+        soft_max(3)
+        store(3, 0, 1024)
+        store(2, 0, 1024)
+        base(4, 512, 512, "y", 3)
+        soft_exp(3)
+        lora(4, 0, 512)
+        lora(4, 512, 512)
+        soft_scale(3)
+        empty(4, 0, 512)
+        down(7)
+        empty(4, 512, 512)
+        turn_gates(3)
+        quantize_z(5)
+        store(4, 0, 1024)
+        base(5, 0, 512, "y", 3)
+        store(1, 0, 1024)
+        copy_gates(3)
+        gate(7)
+        base(5, 512, 512, "y", 3)
+        gate(6)
+        lora(5, 0, 512)
+        lora(5, 512, 512)
+        empty(5, 0, 512)
+        quantize_z(7)
+        base(6, 0, 512, "tr", 2)
+        quantize_z(6)
+        empty(5, 512, 512)
+        base(6, 512, 512, "tr", 2)
+        store(5, 0, 1024)
+        lora(6, 0, 512)
+        lora(6, 512, 512)
+        empty(6, 0, 512)
+        base(7, 0, 512, "y", 3)
+        empty(6, 512, 512)
+        lora(7, 0, 512)
+        store(6, 0, 1024)
+        base(7, 512, 256, "y", 3)
+        empty(7, 0, 512)
+        lora(7, 512, 256)
+        base(7, 768, 256, "y", 3)
+        empty(7, 512, 256)
+        lora(7, 768, 256)
+        store(7, 512, 256)
+        empty(7, 768, 256)
+        store(7, 0, 512)
+        store(7, 768, 256)

@@ -22,11 +22,9 @@ ACT = mybir.ActivationFunctionType
 P = 128
 TILES = 8
 PAIRS = 4
-S_BLOCKS = {0: (2, 3, 7), 1: (2, 3, 7), 2: (1, 3, 5, 7), 3: (1, 3, 5, 7)}
-CONTIG = (4, 5, 6, 7)
-G_A = ()
+S_BLOCKS = ((3, 6, 7), (3, 6, 7), (1, 3, 5, 7), (1, 3, 5, 7), (3, 7), (3, 7), (3, 7), (3, 7))
+CONTIG = ()
 Y_V = ((2, 512), (4, 512), (6, 512), (7, 512))
-G_B = (0, 1, 2, 3)
 
 
 def tile_rankwisemoloradenserouter_d2p_kernel(
@@ -57,15 +55,26 @@ def tile_rankwisemoloradenserouter_d2p_kernel(
         ident = keep.tile([P, P], F32, name="ident")
         nc.vector.memset(ident[:], 0.0)
         scale_cols = keep.tile([P, 8], F32, name="scale_cols")
-        xb = [keep.tile([P, 2, D], U8, align_bytes=64, name=f"xb{h}") for h in range(PAIRS)]
+        xb0 = [keep.tile([P, D], U8, align_bytes=64, name=f"xb0_{r}") for r in range(2)]
+        xb = [keep.tile([P, 2, D], U8, align_bytes=64, name=f"xb{h}") for h in range(1, PAIRS)]
+
+        def x_rows(r):
+            return xb0[r][:] if r < 2 else xb[r // 2 - 1][:, r % 2, :]
+
+        def load_x_tile(r):
+            nc.sync.dma_start(out=xb0[r][:], in_=x_view[:, r, :])
         wr_c = keep.tile([P, 2, E], I32, align_bytes=64, name="wr_c")
         a_raw = keep.tile([P, 2, R], I32, align_bytes=64, name="a_raw")
         b_c = keep.tile([P, F], I32, align_bytes=64, name="b_c")
-        br_bc = keep.tile([P, E], BF16, name="br_bc")
+        br_bc = keep.tile([P, E], F32, name="br_bc")
+        ones = keep.tile([P, P], BF16, align_bytes=64, name="ones")
+        br_rows = keep.tile([P, E], BF16, align_bytes=64, name="br_rows")
+        nc.vector.memset(br_rows[:], 0.0)
+        nc.vector.memset(ones[:], 1.0)
         w0_c = [keep.tile([P, 2, 512], I32, align_bytes=64, name=f"w0_c{f}") for f in range(2)]
 
         def load_x(h):
-            nc.sync.dma_start(out=xb[h][:], in_=x_view[:, 2 * h : 2 * h + 2, :])
+            nc.sync.dma_start(out=xb[h - 1][:], in_=x_view[:, 2 * h : 2 * h + 2, :])
 
         def load_w0(f):
             nc.sync.dma_start(out=w0_c[f][:], in_=w0_view[:, :, 2048 * f : 2048 * f + 2048].bitcast(I32))
@@ -92,30 +101,27 @@ def tile_rankwisemoloradenserouter_d2p_kernel(
                 out=b_sc[32 * q : 32 * q + 4, :].bitcast(I32), in_=b_scales[0, 4 * q : 4 * q + 4, :].bitcast(I32)
             )
 
-        load_x(0)
-        nc.sync.dma_start(out=scale_cols[:], in_=x_scale.unsqueeze(1).to_broadcast([8, 16, 8]))
-        for q in G_A:
-            a_scale(nc.gpsimd, q)
         make_identity(nc, ident[:], nomemset=True)
-        nc.gpsimd.dma_start(out=br_bc[:], in_=br.partition_broadcast(P))
-        for q in G_B:
-            b_scale(nc.gpsimd, q)
-        for q in range(4):
+        nc.sync.dma_start(out=scale_cols[:], in_=x_scale.unsqueeze(1).to_broadcast([8, 16, 8]))
+        load_x_tile(0)
+        for q in range(2):
             wr_scale(nc.sync, q)
-        nc.sync.dma_start(out=wr_c[:], in_=wr_words.rearrange("g p n t -> p g (n t)").bitcast(I32))
+        load_x_tile(1)
+        for q in range(2, 4):
+            wr_scale(nc.sync, q)
         nc.sync.dma_start(out=a_raw[:], in_=a_words.rearrange("g p n t -> p g (n t)").bitcast(I32))
+        nc.sync.dma_start(out=br_rows[0:1, :], in_=br.unsqueeze(0))
         for q in range(4):
-            if q not in G_A:
-                a_scale(nc.sync, q)
+            a_scale(nc.sync, q)
+        nc.sync.dma_start(out=wr_c[:], in_=wr_words.rearrange("g p n t -> p g (n t)").bitcast(I32))
         load_x(1)
-        load_w0(0)
-        load_w0(1)
         for q in range(4):
             w0_scale(nc.sync, q)
+        load_w0(0)
+        load_w0(1)
         nc.sync.dma_start(out=b_c[:], in_=b_words[0].rearrange("p n t -> p (n t)").bitcast(I32))
         for q in range(4):
-            if q not in G_B:
-                b_scale(nc.sync, q)
+            b_scale(nc.sync, q)
         load_x(2)
         load_x(3)
 
@@ -149,10 +155,10 @@ def tile_rankwisemoloradenserouter_d2p_kernel(
                     dest = xw[r][:].rearrange("p (g u q e) -> p g q u e", g=2, u=2, e=2)[
                         :, j // 4, 32 * (j % 4) : 32 * (j % 4) + 32
                     ]
-                    source = xb[r // 2][:, r % 2, cols].bitcast(FP8).rearrange("p (q u e) -> p q u e", u=2, e=2)
+                    source = x_rows(r)[:, cols].bitcast(FP8).rearrange("p (q u e) -> p q u e", u=2, e=2)
                 elif j not in S_BLOCKS[r]:
                     dest = xw[r][:, cols]
-                    source = xb[r // 2][:, r % 2, cols].bitcast(FP8)
+                    source = x_rows(r)[:, cols].bitcast(FP8)
                 else:
                     continue
                 nc.vector.tensor_scalar(
@@ -165,7 +171,7 @@ def tile_rankwisemoloradenserouter_d2p_kernel(
                     cols = slice(P * j, P * j + P)
                     nc.scalar.activation(
                         out=xw[r][:, cols],
-                        in_=xb[r // 2][:, r % 2, cols].bitcast(FP8),
+                        in_=x_rows(r)[:, cols].bitcast(FP8),
                         func=ACT.Copy,
                         scale=scale_cols[:, j : j + 1],
                     )
@@ -181,11 +187,24 @@ def tile_rankwisemoloradenserouter_d2p_kernel(
                         part = words[:, 256 * g + u : 256 * (g + 1) : 2]
                     nc.tensor.transpose(t_ps[r][:, 2 * g + u, :], part, ident[:])
 
-        def interleave(r):
+        def interleave(r, g):
+            nc.scalar.copy(
+                out=xg[r][:, 512 * g : 512 * g + 512].bitcast(F32).rearrange("p (n u) -> p n u", u=2),
+                in_=t_ps[r][:, 2 * g : 2 * g + 2, :].rearrange("p u n -> p n u"),
+            )
+
+        def interleave_tile(r):
             nc.scalar.copy(
                 out=xg[r][:].bitcast(F32).rearrange("p (g n u) -> p g n u", g=2, u=2),
                 in_=t_ps[r][:].rearrange("p (g u) n -> p g n u", g=2),
             )
+
+        def spread_bias():
+            b_ps = l_ps["bias"] = psum.tile([P, E], F32, tag="lg", bufs=1, name="b_ps")
+            nc.tensor.matmul(b_ps[:], lhsT=ones[:], rhs=br_rows[:], start=True, stop=True)
+
+        def copy_bias():
+            nc.scalar.copy(out=br_bc[:], in_=l_ps["bias"][:])
 
         def quantize_x(r):
             nc.vector.quantize_mx(out=xq[r][:].bitcast(FP8X4), scales=xs[r][:], in_=xg[r][:])
@@ -321,28 +340,32 @@ def tile_rankwisemoloradenserouter_d2p_kernel(
         turn(0)
         widen_vector(1)
         widen_scalar(1)
-        perm_words()
         turn(1)
-        interleave(0)
+        interleave(0, 0)
+        interleave(0, 1)
         quantize_x(0)
-        interleave(1)
-        perm_scales()
-        logits(0)
-        widen_scalar(3)
+        interleave(1, 0)
+        spread_bias()
+        perm_words()
+        interleave(1, 1)
+        copy_bias()
         quantize_x(1)
+        logits(0)
+        perm_scales()
+        logits(1)
         widen_scalar(2)
         widen_vector(2)
-        logits(1)
         down(0)
         soft_max(0)
+        widen_scalar(3)
         turn(2)
         widen_vector(3)
         soft_exp(0)
         turn(3)
         soft_scale(0)
-        interleave(2)
+        interleave_tile(2)
         turn_gates(0)
-        interleave(3)
+        interleave_tile(3)
         down(1)
         quantize_x(2)
         copy_gates(0)
@@ -353,117 +376,121 @@ def tile_rankwisemoloradenserouter_d2p_kernel(
         logits(3)
         gate(1)
         base(0, 512, 512, "y", 3)
-        quantize_z(0)
+        widen_scalar(4)
         down(2)
         soft_max(1)
+        widen_scalar(5)
         down(3)
-        widen_vector(4)
+        quantize_z(0)
         soft_exp(1)
+        widen_vector(4)
         lora(0, 0, 512)
+        widen_scalar(7)
         lora(0, 512, 512)
         soft_scale(1)
         turn(4)
-        empty(0, 512, 512)
+        empty(0, 0, 512)
         widen_vector(5)
         turn_gates(1)
-        base(1, 0, 512, "y", 3)
-        copy_gates(1)
-        quantize_z(1)
-        empty(0, 0, 512)
-        gate(2)
         turn(5)
-        interleave(4)
-        store(0, 0, 1024)
-        base(1, 512, 512, "y", 3)
+        quantize_z(1)
+        copy_gates(1)
+        base(1, 0, 512, "y", 3)
+        interleave_tile(4)
         gate(3)
-        interleave(5)
+        base(1, 512, 512, "y", 3)
+        interleave_tile(5)
         quantize_x(4)
         lora(1, 0, 512)
-        lora(1, 512, 512)
+        empty(0, 512, 512)
         quantize_x(5)
-        empty(1, 0, 512)
-        base(2, 0, 512, "y", 3)
-        widen_vector(6)
+        lora(1, 512, 512)
+        gate(2)
         logits(4)
+        empty(1, 0, 512)
         logits(5)
-        down(4)
-        soft_max(2)
-        down(5)
-        quantize_z(2)
-        soft_exp(2)
-        base(2, 512, 512, "y", 3)
+        base(2, 0, 512, "y", 3)
         empty(1, 512, 512)
-        soft_scale(2)
+        base(2, 512, 512, "y", 3)
+        quantize_z(2)
+        soft_max(2)
+        widen_scalar(6)
+        store(1, 0, 1024)
         lora(2, 0, 512)
-        widen_vector(7)
+        store(0, 0, 1024)
         lora(2, 512, 512)
+        widen_vector(6)
+        down(4)
+        soft_exp(2)
         empty(2, 0, 512)
+        down(5)
+        soft_scale(2)
+        widen_vector(7)
         turn_gates(2)
-        quantize_z(3)
         turn(6)
         empty(2, 512, 512)
         copy_gates(2)
         turn(7)
-        interleave(6)
-        base(3, 0, 512, "y", 3)
         gate(4)
-        interleave(7)
+        interleave_tile(6)
+        base(3, 0, 512, "y", 3)
+        interleave_tile(7)
         quantize_x(6)
         base(3, 512, 512, "y", 3)
+        quantize_z(3)
         quantize_x(7)
         lora(3, 0, 512)
-        quantize_z(4)
-        lora(3, 512, 512)
         gate(5)
-        empty(3, 0, 512)
-        down(6)
-        empty(3, 512, 512)
         logits(6)
+        lora(3, 512, 512)
+        empty(3, 0, 512)
         logits(7)
         base(4, 0, 512, "y", 3)
+        quantize_z(4)
+        empty(3, 512, 512)
         soft_max(3)
-        store(3, 0, 1024)
-        store(2, 0, 1024)
         base(4, 512, 512, "y", 3)
-        soft_exp(3)
+        store(3, 0, 1024)
         lora(4, 0, 512)
+        soft_exp(3)
         lora(4, 512, 512)
-        soft_scale(3)
+        down(6)
         empty(4, 0, 512)
-        down(7)
+        soft_scale(3)
+        base(5, 0, 512, "y", 3)
         empty(4, 512, 512)
-        turn_gates(3)
+        base(5, 512, 512, "y", 3)
         quantize_z(5)
         store(4, 0, 1024)
-        base(5, 0, 512, "y", 3)
-        store(1, 0, 1024)
+        store(2, 0, 1024)
+        turn_gates(3)
+        down(7)
         copy_gates(3)
-        gate(7)
-        base(5, 512, 512, "y", 3)
-        gate(6)
         lora(5, 0, 512)
+        gate(6)
         lora(5, 512, 512)
-        empty(5, 0, 512)
-        quantize_z(7)
         base(6, 0, 512, "tr", 2)
+        empty(5, 0, 512)
         quantize_z(6)
-        empty(5, 512, 512)
         base(6, 512, 512, "tr", 2)
-        store(5, 0, 1024)
+        empty(5, 512, 512)
+        gate(7)
         lora(6, 0, 512)
+        store(5, 0, 1024)
         lora(6, 512, 512)
-        empty(6, 0, 512)
         base(7, 0, 512, "y", 3)
+        quantize_z(7)
+        empty(6, 0, 512)
         empty(6, 512, 512)
         lora(7, 0, 512)
-        store(6, 0, 1024)
         base(7, 512, 256, "y", 3)
-        empty(7, 0, 512)
+        store(6, 0, 1024)
         lora(7, 512, 256)
+        empty(7, 0, 512)
         base(7, 768, 256, "y", 3)
-        empty(7, 512, 256)
         lora(7, 768, 256)
-        store(7, 512, 256)
+        empty(7, 512, 256)
         empty(7, 768, 256)
-        store(7, 0, 512)
+        store(7, 512, 256)
         store(7, 768, 256)
+        store(7, 0, 512)

@@ -46,7 +46,6 @@ def tile_rankwisemoloradenserouter_d2p_kernel(
         zero_col = keep.tile([P, 1], F32, name="zero_col")
         exp_col = keep.tile([P, 1], F32, name="exp_col")
         nc.vector.memset(zero_col[:], 0.0)
-        nc.scalar.activation(out=exp_col[:], in_=zero_col[:], func=ACT.Exp)
 
         x_view = x_bytes.rearrange("(p r) k -> p r k", r=TILES)
         out_view = out.rearrange("(p r) f -> p r f", r=TILES)
@@ -102,27 +101,34 @@ def tile_rankwisemoloradenserouter_d2p_kernel(
             )
 
         make_identity(nc, ident[:], nomemset=True)
-        nc.sync.dma_start(out=scale_cols[:], in_=x_scale.unsqueeze(1).to_broadcast([8, 16, 8]))
+        nc.scalar.dma_start(out=scale_cols[:], in_=x_scale.unsqueeze(1).to_broadcast([8, 16, 8]))
+        nc.scalar.activation(out=exp_col[:], in_=zero_col[:], func=ACT.Exp)
         load_x_tile(0)
-        for q in range(2):
-            wr_scale(nc.sync, q)
         load_x_tile(1)
-        for q in range(2, 4):
-            wr_scale(nc.sync, q)
-        nc.sync.dma_start(out=a_raw[:], in_=a_words.rearrange("g p n t -> p g (n t)").bitcast(I32))
-        nc.sync.dma_start(out=br_rows[0:1, :], in_=br.unsqueeze(0))
-        for q in range(4):
-            a_scale(nc.sync, q)
+        wr_scale(nc.sync, 0)
+        wr_scale(nc.sync, 1)
+        a_scale(nc.sync, 0)
         nc.sync.dma_start(out=wr_c[:], in_=wr_words.rearrange("g p n t -> p g (n t)").bitcast(I32))
+        nc.sync.dma_start(out=a_raw[:], in_=a_words.rearrange("g p n t -> p g (n t)").bitcast(I32))
+        wr_scale(nc.sync, 2)
+        wr_scale(nc.sync, 3)
+        nc.sync.dma_start(out=br_rows[0:1, :], in_=br.unsqueeze(0))
+        a_scale(nc.sync, 1)
+        a_scale(nc.sync, 2)
+        a_scale(nc.sync, 3)
         load_x(1)
-        for q in range(4):
-            w0_scale(nc.sync, q)
+        load_x(2)
         load_w0(0)
+        w0_scale(nc.sync, 0)
+        w0_scale(nc.sync, 1)
+        w0_scale(nc.sync, 2)
+        w0_scale(nc.sync, 3)
         load_w0(1)
         nc.sync.dma_start(out=b_c[:], in_=b_words[0].rearrange("p n t -> p (n t)").bitcast(I32))
-        for q in range(4):
-            b_scale(nc.sync, q)
-        load_x(2)
+        b_scale(nc.sync, 0)
+        b_scale(nc.sync, 1)
+        b_scale(nc.sync, 2)
+        b_scale(nc.sync, 3)
         load_x(3)
 
         xw = [keep.tile([P, D], BF16, align_bytes=64, name=f"xw{r}") for r in range(TILES)]
@@ -148,8 +154,8 @@ def tile_rankwisemoloradenserouter_d2p_kernel(
         g_ps = {}
         t_ps = {}
 
-        def widen_vector(r):
-            for j in range(8):
+        def widen_vector(r, g):
+            for j in range(4 * g, 4 * g + 4):
                 cols = slice(P * j, P * j + P)
                 if r in CONTIG:
                     dest = xw[r][:].rearrange("p (g u q e) -> p g q u e", g=2, u=2, e=2)[
@@ -200,7 +206,7 @@ def tile_rankwisemoloradenserouter_d2p_kernel(
             )
 
         def spread_bias():
-            b_ps = l_ps["bias"] = psum.tile([P, E], F32, tag="lg", bufs=1, name="b_ps")
+            b_ps = l_ps["bias"] = psum.tile([P, E], F32, tag="y", bufs=3, name="b_ps")
             nc.tensor.matmul(b_ps[:], lhsT=ones[:], rhs=br_rows[:], start=True, stop=True)
 
         def copy_bias():
@@ -243,10 +249,12 @@ def tile_rankwisemoloradenserouter_d2p_kernel(
                         stop=(g == 1),
                     )
 
-        def soft_max(h):
+        def soft_add(h):
             nc.vector.tensor_tensor(
                 out=lb[h][:], in0=l_ps[h][:], in1=br_bc[:].unsqueeze(1).to_broadcast([P, 2, E]), op=ADD
             )
+
+        def soft_peak(h):
             nc.vector.tensor_reduce(out=nm[h][:], in_=lb[h][:], axis=AX, op=MAX, negate=True)
 
         def soft_exp(h):
@@ -259,8 +267,10 @@ def tile_rankwisemoloradenserouter_d2p_kernel(
                     accum_out=sm[h][:, i : i + 1],
                 )
 
-        def soft_scale(h):
+        def soft_recip(h):
             nc.vector.reciprocal(out=rs[h][:], in_=sm[h][:])
+
+        def soft_scale(h):
             for i in range(2):
                 nc.vector.tensor_scalar(
                     out=gt[h][:, i, :],
@@ -335,162 +345,106 @@ def tile_rankwisemoloradenserouter_d2p_kernel(
             base(r, 0, 512, tag, bufs)
             base(r, 512, 512, tag, bufs)
 
-        widen_vector(0)
-        widen_scalar(0)
-        turn(0)
-        widen_vector(1)
-        widen_scalar(1)
-        turn(1)
-        interleave(0, 0)
-        interleave(0, 1)
-        quantize_x(0)
-        interleave(1, 0)
+        def widen(r):
+            widen_vector(r, 0)
+            widen_vector(r, 1)
+
+        def bases(r, tag, bufs):
+            base(r, 0, 512, tag, bufs)
+            base(r, 512, 512, tag, bufs)
+
+        def out_half(r, c0):
+            empty(r, c0, 512)
+
+        for r in (0, 1):
+            widen(r)
+            widen_scalar(r)
+            turn(r)
+        for r in (0, 1):
+            interleave(r, 0)
+            interleave(r, 1)
         spread_bias()
         perm_words()
-        interleave(1, 1)
-        copy_bias()
+        quantize_x(0)
         quantize_x(1)
-        logits(0)
         perm_scales()
+        copy_bias()
+        logits(0)
         logits(1)
+        soft_add(0)
+        widen_vector(2, 0)
+        soft_peak(0)
         widen_scalar(2)
-        widen_vector(2)
-        down(0)
-        soft_max(0)
         widen_scalar(3)
-        turn(2)
-        widen_vector(3)
         soft_exp(0)
-        turn(3)
+        widen_vector(2, 1)
+        widen(3)
+        soft_recip(0)
         soft_scale(0)
-        interleave_tile(2)
+        down(0)
+        turn(2)
+        turn(3)
         turn_gates(0)
+        interleave_tile(2)
         interleave_tile(3)
+        copy_gates(0)
         down(1)
         quantize_x(2)
-        copy_gates(0)
         quantize_x(3)
-        base(0, 0, 512, "y", 3)
         gate(0)
-        logits(2)
-        logits(3)
         gate(1)
-        base(0, 512, 512, "y", 3)
-        widen_scalar(4)
-        down(2)
-        soft_max(1)
-        widen_scalar(5)
-        down(3)
-        quantize_z(0)
-        soft_exp(1)
-        widen_vector(4)
-        lora(0, 0, 512)
-        widen_scalar(7)
-        lora(0, 512, 512)
-        soft_scale(1)
-        turn(4)
-        empty(0, 0, 512)
-        widen_vector(5)
-        turn_gates(1)
-        turn(5)
-        quantize_z(1)
-        copy_gates(1)
-        base(1, 0, 512, "y", 3)
-        interleave_tile(4)
-        gate(3)
-        base(1, 512, 512, "y", 3)
-        interleave_tile(5)
-        quantize_x(4)
-        lora(1, 0, 512)
-        empty(0, 512, 512)
-        quantize_x(5)
-        lora(1, 512, 512)
-        gate(2)
-        logits(4)
-        empty(1, 0, 512)
-        logits(5)
-        base(2, 0, 512, "y", 3)
-        empty(1, 512, 512)
-        base(2, 512, 512, "y", 3)
-        quantize_z(2)
-        soft_max(2)
-        widen_scalar(6)
-        store(1, 0, 1024)
-        lora(2, 0, 512)
-        store(0, 0, 1024)
-        lora(2, 512, 512)
-        widen_vector(6)
-        down(4)
-        soft_exp(2)
-        empty(2, 0, 512)
-        down(5)
-        soft_scale(2)
-        widen_vector(7)
-        turn_gates(2)
-        turn(6)
-        empty(2, 512, 512)
-        copy_gates(2)
-        turn(7)
-        gate(4)
-        interleave_tile(6)
-        base(3, 0, 512, "y", 3)
-        interleave_tile(7)
-        quantize_x(6)
-        base(3, 512, 512, "y", 3)
-        quantize_z(3)
-        quantize_x(7)
-        lora(3, 0, 512)
-        gate(5)
-        logits(6)
-        lora(3, 512, 512)
-        empty(3, 0, 512)
-        logits(7)
-        base(4, 0, 512, "y", 3)
-        quantize_z(4)
-        empty(3, 512, 512)
-        soft_max(3)
-        base(4, 512, 512, "y", 3)
-        store(3, 0, 1024)
-        lora(4, 0, 512)
-        soft_exp(3)
-        lora(4, 512, 512)
-        down(6)
-        empty(4, 0, 512)
-        soft_scale(3)
-        base(5, 0, 512, "y", 3)
-        empty(4, 512, 512)
-        base(5, 512, 512, "y", 3)
-        quantize_z(5)
-        store(4, 0, 1024)
-        store(2, 0, 1024)
-        turn_gates(3)
-        down(7)
-        copy_gates(3)
-        lora(5, 0, 512)
-        gate(6)
-        lora(5, 512, 512)
-        base(6, 0, 512, "tr", 2)
-        empty(5, 0, 512)
+        for h in range(PAIRS - 1):
+            r0, r1 = 2 * h, 2 * h + 1
+            ahead = range(2 * h + 4, 2 * h + 6) if h + 2 < PAIRS else ()
+            base(r0, 0, 512, "y", 3)
+            logits(r0 + 2)
+            logits(r1 + 2)
+            soft_add(h + 1)
+            quantize_z(r0)
+            soft_peak(h + 1)
+            quantize_z(r1)
+            for r in ahead:
+                widen_scalar(r)
+            for r in ahead[:1]:
+                widen(r)
+            soft_exp(h + 1)
+            soft_recip(h + 1)
+            soft_scale(h + 1)
+            for r in ahead[1:]:
+                widen(r)
+            base(r0, 512, 512, "y", 3)
+            down(r0 + 2)
+            down(r1 + 2)
+            lora(r0, 0, 512)
+            lora(r0, 512, 512)
+            empty(r0, 0, 512)
+            base(r1, 0, 512, "y", 3)
+            turn_gates(h + 1)
+            copy_gates(h + 1)
+            empty(r0, 512, 512)
+            store(r0, 0, F)
+            for r in ahead:
+                turn(r)
+                interleave_tile(r)
+            gate(r0 + 2)
+            for r in ahead:
+                quantize_x(r)
+            gate(r1 + 2)
+            base(r1, 512, 512, "y", 3)
+            lora(r1, 0, 512)
+            lora(r1, 512, 512)
+            empty(r1, 0, 512)
+            empty(r1, 512, 512)
+            store(r1, 0, F)
         quantize_z(6)
-        base(6, 512, 512, "tr", 2)
-        empty(5, 512, 512)
-        gate(7)
-        lora(6, 0, 512)
-        store(5, 0, 1024)
-        lora(6, 512, 512)
-        base(7, 0, 512, "y", 3)
         quantize_z(7)
-        empty(6, 0, 512)
-        empty(6, 512, 512)
-        lora(7, 0, 512)
-        base(7, 512, 256, "y", 3)
-        store(6, 0, 1024)
-        lora(7, 512, 256)
-        empty(7, 0, 512)
-        base(7, 768, 256, "y", 3)
-        lora(7, 768, 256)
-        empty(7, 512, 256)
-        empty(7, 768, 256)
-        store(7, 512, 256)
-        store(7, 768, 256)
-        store(7, 0, 512)
+        bases(6, "tr", 2)
+        for c0 in (0, 512):
+            lora(6, c0, 512)
+            empty(6, c0, 512)
+            store(6, c0, 512)
+        for c0, width in ((0, 512), (512, 256), (768, 256)):
+            base(7, c0, width, "y", 3)
+            lora(7, c0, width)
+            empty(7, c0, width)
+            store(7, c0, width)

from contextlib import ExitStack

import concourse.mybir as mybir
from concourse.masks import make_identity

T, D, F, E, R = 1024, 1024, 1024, 128, 512
FLOPS = 2 * T * D * (F + E + R) + 2 * T * R * F

F32 = mybir.dt.float32
BF16 = mybir.dt.bfloat16
I32 = mybir.dt.int32
U32 = mybir.dt.uint32
U8 = mybir.dt.uint8
FP8 = mybir.dt.float8_e4m3fn
FP8X4 = mybir.dt.float8_e4m3fn_x4
MULT = mybir.AluOpType.mult
ADD = mybir.AluOpType.add
MAX = mybir.AluOpType.max
AX = mybir.AxisListType.X
ACT = mybir.ActivationFunctionType

P = 128
TILES = 8
PAIRS = 4
S_BLOCKS = ((3, 6, 7), (3, 6, 7), (1, 3, 5, 7), (1, 3, 5, 7), (3, 7), (3, 7), (3, 7), (3, 7))
CONTIG = ()
Y_V = ((2, 512), (4, 512), (6, 512), (7, 512))


def tile_rankwisemoloradenserouter_d2p_kernel(
    tc, x_bytes, x_scale, w0_words, w0_scales, wr_words, wr_scales, br, a_words, a_scales, b_words, b_scales, out
):
    nc = tc.nc
    with ExitStack() as ctx:
        keep = ctx.enter_context(tc.tile_pool(name="keep", bufs=1))
        psum = ctx.enter_context(tc.psum_pool(name="psum", bufs=1))
        ctx.enter_context(tc.manual_schedule())

        a_sc_raw = keep.tile([P, 2 * R], U8, align_bytes=64, name="a_sc_raw")
        wr_sc = keep.tile([P, 2, E], U8, align_bytes=64, name="wr_sc")
        w0_sc = keep.tile([P, F], U8, align_bytes=64, name="w0_sc")
        b_sc = keep.tile([P, F], U8, align_bytes=64, name="b_sc")
        for sc in (a_sc_raw[:], wr_sc[:].rearrange("p g n -> p (g n)"), w0_sc[:], b_sc[:]):
            nc.vector.memset(sc.bitcast(I32), 0)

        zero_col = keep.tile([P, 1], F32, name="zero_col")
        exp_col = keep.tile([P, 1], F32, name="exp_col")
        nc.vector.memset(zero_col[:], 0.0)

        x_view = x_bytes.rearrange("(p r) k -> p r k", r=TILES)
        out_view = out.rearrange("(p r) f -> p r f", r=TILES)
        w0_view = w0_words.rearrange("g p n t -> p g (n t)")

        ident = keep.tile([P, P], F32, name="ident")
        nc.vector.memset(ident[:], 0.0)
        scale_cols = keep.tile([P, 8], F32, name="scale_cols")
        xb0 = [keep.tile([P, D], U8, align_bytes=64, name=f"xb0_{r}") for r in range(2)]
        xb = [keep.tile([P, 2, D], U8, align_bytes=64, name=f"xb{h}") for h in range(1, PAIRS)]

        def x_rows(r):
            return xb0[r][:] if r < 2 else xb[r // 2 - 1][:, r % 2, :]

        def load_x_tile(r):
            nc.sync.dma_start(out=xb0[r][:], in_=x_view[:, r, :])
        wr_c = keep.tile([P, 2, E], I32, align_bytes=64, name="wr_c")
        a_raw = keep.tile([P, 2, R], I32, align_bytes=64, name="a_raw")
        b_c = keep.tile([P, F], I32, align_bytes=64, name="b_c")
        br_bc = keep.tile([P, E], F32, name="br_bc")
        ones = keep.tile([P, P], BF16, align_bytes=64, name="ones")
        br_rows = keep.tile([P, E], BF16, align_bytes=64, name="br_rows")
        nc.vector.memset(br_rows[:], 0.0)
        nc.vector.memset(ones[:], 1.0)
        w0_c = [keep.tile([P, 2, 512], I32, align_bytes=64, name=f"w0_c{f}") for f in range(2)]

        def load_x(h):
            nc.sync.dma_start(out=xb[h - 1][:], in_=x_view[:, 2 * h : 2 * h + 2, :])

        def load_w0(f):
            nc.sync.dma_start(out=w0_c[f][:], in_=w0_view[:, :, 2048 * f : 2048 * f + 2048].bitcast(I32))

        def wr_scale(queue, q):
            queue.dma_start(
                out=wr_sc[32 * q : 32 * q + 4, :, :].bitcast(I32),
                in_=wr_scales[:, 4 * q : 4 * q + 4, :].bitcast(I32).rearrange("g q n -> q g n"),
            )

        def a_scale(queue, q):
            queue.dma_start(
                out=a_sc_raw[32 * q : 32 * q + 4, :].bitcast(I32).rearrange("p (g n) -> p g n", g=2),
                in_=a_scales[:, 4 * q : 4 * q + 4, :].bitcast(I32).rearrange("g q n -> q g n"),
            )

        def w0_scale(queue, q):
            queue.dma_start(
                out=w0_sc[32 * q : 32 * q + 8, :].bitcast(I32), in_=w0_scales[:, 4 * q : 4 * q + 4, :].bitcast(I32)
            )

        def b_scale(queue, q):
            queue.dma_start(
                out=b_sc[32 * q : 32 * q + 4, :].bitcast(I32), in_=b_scales[0, 4 * q : 4 * q + 4, :].bitcast(I32)
            )

        make_identity(nc, ident[:], nomemset=True)
        nc.scalar.dma_start(out=scale_cols[:], in_=x_scale.unsqueeze(1).to_broadcast([8, 16, 8]))
        nc.scalar.activation(out=exp_col[:], in_=zero_col[:], func=ACT.Exp)
        load_x_tile(0)
        load_x_tile(1)
        wr_scale(nc.sync, 0)
        wr_scale(nc.sync, 1)
        a_scale(nc.sync, 0)
        nc.sync.dma_start(out=wr_c[:], in_=wr_words.rearrange("g p n t -> p g (n t)").bitcast(I32))
        nc.sync.dma_start(out=a_raw[:], in_=a_words.rearrange("g p n t -> p g (n t)").bitcast(I32))
        wr_scale(nc.sync, 2)
        wr_scale(nc.sync, 3)
        nc.sync.dma_start(out=br_rows[0:1, :], in_=br.unsqueeze(0))
        a_scale(nc.sync, 1)
        a_scale(nc.sync, 2)
        a_scale(nc.sync, 3)
        load_x(1)
        load_x(2)
        load_w0(0)
        w0_scale(nc.sync, 0)
        w0_scale(nc.sync, 1)
        w0_scale(nc.sync, 2)
        w0_scale(nc.sync, 3)
        load_w0(1)
        nc.sync.dma_start(out=b_c[:], in_=b_words[0].rearrange("p n t -> p (n t)").bitcast(I32))
        b_scale(nc.sync, 0)
        b_scale(nc.sync, 1)
        b_scale(nc.sync, 2)
        b_scale(nc.sync, 3)
        load_x(3)

        xw = [keep.tile([P, D], BF16, align_bytes=64, name=f"xw{r}") for r in range(TILES)]
        xg = [keep.tile([P, 2 * P * 4], BF16, align_bytes=64, name=f"xg{r}") for r in range(TILES)]
        xq = [keep.tile([P, 2 * P], U32, align_bytes=64, name=f"xq{r}") for r in range(TILES)]
        xs = [keep.tile([P, 2 * P], U8, align_bytes=64, name=f"xs{r}") for r in range(TILES)]
        zb = [keep.tile([P, P, 4], BF16, align_bytes=64, name=f"zb{r}") for r in range(TILES)]
        zq = [keep.tile([P, P], U32, align_bytes=64, name=f"zq{r}") for r in range(TILES)]
        zs = [keep.tile([P, P], U8, align_bytes=64, name=f"zs{r}") for r in range(TILES)]
        yo = [keep.tile([P, F], F32, align_bytes=64, name=f"yo{r}") for r in range(TILES)]
        lb = [keep.tile([P, 2, E], F32, name=f"lb{h}") for h in range(PAIRS)]
        ex = [keep.tile([P, 2, E], F32, name=f"ex{h}") for h in range(PAIRS)]
        gt = [keep.tile([P, 2, E], F32, name=f"gt{h}") for h in range(PAIRS)]
        gs = [keep.tile([P, 2, P], F32, name=f"gs{h}") for h in range(PAIRS)]
        nm = [keep.tile([P, 2], F32, name=f"nm{h}") for h in range(PAIRS)]
        sm = [keep.tile([P, 2], F32, name=f"sm{h}") for h in range(PAIRS)]
        rs = [keep.tile([P, 2], F32, name=f"rs{h}") for h in range(PAIRS)]
        a_c = keep.tile([P, 2, 4, P], I32, align_bytes=64, name="a_c")
        a_sc = keep.tile([P, 2, 4, P], U8, align_bytes=64, name="a_sc")
        u_ps = {}
        y_ps = {}
        l_ps = {}
        g_ps = {}
        t_ps = {}

        def widen_vector(r, g):
            for j in range(4 * g, 4 * g + 4):
                cols = slice(P * j, P * j + P)
                if r in CONTIG:
                    dest = xw[r][:].rearrange("p (g u q e) -> p g q u e", g=2, u=2, e=2)[
                        :, j // 4, 32 * (j % 4) : 32 * (j % 4) + 32
                    ]
                    source = x_rows(r)[:, cols].bitcast(FP8).rearrange("p (q u e) -> p q u e", u=2, e=2)
                elif j not in S_BLOCKS[r]:
                    dest = xw[r][:, cols]
                    source = x_rows(r)[:, cols].bitcast(FP8)
                else:
                    continue
                nc.vector.tensor_scalar(
                    out=dest, in0=source, scalar1=scale_cols[:, j : j + 1], scalar2=None, op0=MULT
                )

        def widen_scalar(r):
            for j in range(8):
                if r not in CONTIG and j in S_BLOCKS[r]:
                    cols = slice(P * j, P * j + P)
                    nc.scalar.activation(
                        out=xw[r][:, cols],
                        in_=x_rows(r)[:, cols].bitcast(FP8),
                        func=ACT.Copy,
                        scale=scale_cols[:, j : j + 1],
                    )

        def turn(r):
            t_ps[r] = psum.tile([P, 4, P], F32, tag="tr", bufs=2, name=f"t_ps{r}")
            words = xw[r][:].bitcast(F32)
            for g in range(2):
                for u in range(2):
                    if r in CONTIG:
                        part = words[:, 256 * g + P * u : 256 * g + P * u + P]
                    else:
                        part = words[:, 256 * g + u : 256 * (g + 1) : 2]
                    nc.tensor.transpose(t_ps[r][:, 2 * g + u, :], part, ident[:])

        def interleave(r, g):
            nc.scalar.copy(
                out=xg[r][:, 512 * g : 512 * g + 512].bitcast(F32).rearrange("p (n u) -> p n u", u=2),
                in_=t_ps[r][:, 2 * g : 2 * g + 2, :].rearrange("p u n -> p n u"),
            )

        def interleave_tile(r):
            nc.scalar.copy(
                out=xg[r][:].bitcast(F32).rearrange("p (g n u) -> p g n u", g=2, u=2),
                in_=t_ps[r][:].rearrange("p (g u) n -> p g n u", g=2),
            )

        def spread_bias():
            b_ps = l_ps["bias"] = psum.tile([P, E], F32, tag="y", bufs=3, name="b_ps")
            nc.tensor.matmul(b_ps[:], lhsT=ones[:], rhs=br_rows[:], start=True, stop=True)

        def copy_bias():
            nc.scalar.copy(out=br_bc[:], in_=l_ps["bias"][:])

        def quantize_x(r):
            nc.vector.quantize_mx(out=xq[r][:].bitcast(FP8X4), scales=xs[r][:], in_=xg[r][:])

        def xq_of(r, g):
            return xq[r][:, P * g : P * g + P].bitcast(FP8X4), xs[r][:, P * g : P * g + P]

        def logits(r):
            h, i = r // 2, r % 2
            if i == 0:
                l_ps[h] = psum.tile([P, 2, E], F32, tag="lg", bufs=1, name=f"l_ps{h}")
            for g in range(2):
                codes, scales = xq_of(r, g)
                nc.tensor.matmul_mx(
                    out=l_ps[h][:, i, :],
                    lhsT=codes,
                    lhsT_scale=scales,
                    rhs=wr_c[:, g, :].bitcast(FP8X4),
                    rhs_scale=wr_sc[:, g, :],
                    start=(g == 0),
                    stop=(g == 1),
                )

        def down(r):
            u_ps[r] = psum.tile([P, 4, P], F32, tag="u", bufs=2, name=f"u_ps{r}")
            for t in range(4):
                for g in range(2):
                    codes, scales = xq_of(r, g)
                    nc.tensor.matmul_mx(
                        out=u_ps[r][:, t, :],
                        lhsT=a_c[:, g, t, :].bitcast(FP8X4),
                        lhsT_scale=a_sc[:, g, t, :],
                        rhs=codes,
                        rhs_scale=scales,
                        start=(g == 0),
                        stop=(g == 1),
                    )

        def soft_add(h):
            nc.vector.tensor_tensor(
                out=lb[h][:], in0=l_ps[h][:], in1=br_bc[:].unsqueeze(1).to_broadcast([P, 2, E]), op=ADD
            )

        def soft_peak(h):
            nc.vector.tensor_reduce(out=nm[h][:], in_=lb[h][:], axis=AX, op=MAX, negate=True)

        def soft_exp(h):
            for i in range(2):
                nc.scalar.activation(
                    out=ex[h][:, i, :],
                    in_=lb[h][:, i, :],
                    func=ACT.Exp,
                    bias=nm[h][:, i : i + 1],
                    accum_out=sm[h][:, i : i + 1],
                )

        def soft_recip(h):
            nc.vector.reciprocal(out=rs[h][:], in_=sm[h][:])

        def soft_scale(h):
            for i in range(2):
                nc.vector.tensor_scalar(
                    out=gt[h][:, i, :],
                    in0=ex[h][:, i, :],
                    scalar1=rs[h][:, i : i + 1],
                    scalar2=float(E),
                    op0=MULT,
                    op1=MULT,
                )

        def turn_gates(h):
            g_ps[h] = psum.tile([P, 2, P], F32, tag="lg", bufs=1, name=f"g_ps{h}")
            for i in range(2):
                nc.tensor.transpose(g_ps[h][:, i, :], gt[h][:, i, :], ident[:])

        def copy_gates(h):
            nc.scalar.copy(out=gs[h][:], in_=g_ps[h][:])

        def gate(r):
            nc.vector.tensor_tensor(
                out=zb[r][:].rearrange("p (c i) t -> p c t i", i=4),
                in0=u_ps[r][:].rearrange("p t (c i) -> p c t i", i=4),
                in1=gs[r // 2][:, r % 2, :].rearrange("p (c i) -> p c i", i=4).unsqueeze(2).to_broadcast([P, 32, 4, 4]),
                op=MULT,
            )

        def quantize_z(r):
            nc.vector.quantize_mx(
                out=zq[r][:].bitcast(FP8X4), scales=zs[r][:], in_=zb[r][:].rearrange("p n t -> p (n t)")
            )

        def base(r, c0, width, tag, bufs):
            y_ps[r, c0] = psum.tile([P, width], F32, tag=tag, bufs=bufs, name=f"y_ps{r}_{c0}")
            f, c = c0 // 512, c0 % 512
            for g in range(2):
                codes, scales = xq_of(r, g)
                nc.tensor.matmul_mx(
                    out=y_ps[r, c0][:],
                    lhsT=codes,
                    lhsT_scale=scales,
                    rhs=w0_c[f][:, g, c : c + width].bitcast(FP8X4),
                    rhs_scale=w0_sc[4 * g :, c0 : c0 + width],
                    start=(g == 0),
                    stop=False,
                )

        def lora(r, c0, width):
            nc.tensor.matmul_mx(
                out=y_ps[r, c0][:],
                lhsT=zq[r][:].bitcast(FP8X4),
                lhsT_scale=zs[r][:],
                rhs=b_c[:, c0 : c0 + width].bitcast(FP8X4),
                rhs_scale=b_sc[:, c0 : c0 + width],
                start=False,
                stop=True,
            )

        def empty(r, c0, width):
            engine_copy = nc.vector.tensor_copy if (r, c0) in Y_V else nc.scalar.copy
            engine_copy(out=yo[r][:, c0 : c0 + width], in_=y_ps[r, c0][:])

        def store(r, c0, width):
            nc.sync.dma_start(out=out_view[:, r, c0 : c0 + width], in_=yo[r][:, c0 : c0 + width])

        def perm_words():
            nc.vector.tensor_copy(out=a_c[:], in_=a_raw[:].rearrange("p g (m t) -> p g t m", t=4))

        def perm_scales():
            nc.vector.tensor_copy(out=a_sc[:], in_=a_sc_raw[:].rearrange("p (g m t) -> p g t m", g=2, t=4))

        def bases(r, tag, bufs):
            base(r, 0, 512, tag, bufs)
            base(r, 512, 512, tag, bufs)

        def widen(r):
            widen_vector(r, 0)
            widen_vector(r, 1)

        def bases(r, tag, bufs):
            base(r, 0, 512, tag, bufs)
            base(r, 512, 512, tag, bufs)

        def out_half(r, c0):
            empty(r, c0, 512)

        for r in (0, 1):
            widen(r)
            widen_scalar(r)
            turn(r)
        for r in (0, 1):
            interleave(r, 0)
            interleave(r, 1)
        spread_bias()
        perm_words()
        quantize_x(0)
        quantize_x(1)
        perm_scales()
        copy_bias()
        logits(0)
        logits(1)
        soft_add(0)
        widen_vector(2, 0)
        soft_peak(0)
        widen_scalar(2)
        widen_scalar(3)
        soft_exp(0)
        widen_vector(2, 1)
        widen(3)
        soft_recip(0)
        soft_scale(0)
        down(0)
        turn(2)
        turn(3)
        turn_gates(0)
        interleave_tile(2)
        interleave_tile(3)
        copy_gates(0)
        down(1)
        quantize_x(2)
        quantize_x(3)
        gate(0)
        gate(1)
        for h in range(PAIRS - 1):
            r0, r1 = 2 * h, 2 * h + 1
            ahead = range(2 * h + 4, 2 * h + 6) if h + 2 < PAIRS else ()
            base(r0, 0, 512, "y", 3)
            logits(r0 + 2)
            logits(r1 + 2)
            soft_add(h + 1)
            quantize_z(r0)
            soft_peak(h + 1)
            quantize_z(r1)
            for r in ahead:
                widen_scalar(r)
            for r in ahead[:1]:
                widen(r)
            soft_exp(h + 1)
            soft_recip(h + 1)
            soft_scale(h + 1)
            for r in ahead[1:]:
                widen(r)
            base(r0, 512, 512, "y", 3)
            down(r0 + 2)
            down(r1 + 2)
            lora(r0, 0, 512)
            lora(r0, 512, 512)
            empty(r0, 0, 512)
            base(r1, 0, 512, "y", 3)
            turn_gates(h + 1)
            copy_gates(h + 1)
            empty(r0, 512, 512)
            store(r0, 0, F)
            for r in ahead:
                turn(r)
                interleave_tile(r)
            gate(r0 + 2)
            for r in ahead:
                quantize_x(r)
            gate(r1 + 2)
            base(r1, 512, 512, "y", 3)
            lora(r1, 0, 512)
            lora(r1, 512, 512)
            empty(r1, 0, 512)
            empty(r1, 512, 512)
            store(r1, 0, F)
        quantize_z(6)
        quantize_z(7)
        bases(6, "tr", 2)
        for c0 in (0, 512):
            lora(6, c0, 512)
            empty(6, c0, 512)
            store(6, c0, 512)
        for c0, width in ((0, 512), (512, 256), (768, 256)):
            base(7, c0, width, "y", 3)
            lora(7, c0, width)
            empty(7, c0, width)
            store(7, c0, width)
